import numpy as np
import ml_dtypes


def mxq(x, axis, fmt="e4m3"):
    dtype, down = {"e4m3": (ml_dtypes.float8_e4m3fn, 7), "e5m2": (ml_dtypes.float8_e5m2, 14)}[fmt]
    v = np.moveaxis(np.asarray(x, np.float32).astype(ml_dtypes.bfloat16).astype(np.float64), axis, -1)
    blocks = v.reshape(v.shape[:-1] + (-1, 32))
    amax = np.abs(blocks).max(-1, keepdims=True)
    byte = np.maximum(np.where(amax > 0, np.frexp(amax)[1] - 1 + 127, 0) - down, 1)
    scale = np.exp2(byte - 127.0)
    codes = (blocks / scale).astype(np.float32).astype(dtype).astype(np.float64)
    return np.moveaxis((codes * scale).reshape(v.shape), -1, axis)


WIDE = False


def mx_kscale(k):
    if not WIDE:
        return np.ones(k)
    levels = np.array([10, -10, 5, -5, 0])
    if k % 512:
        return np.exp2(np.random.permutation(np.resize(levels, k // 32))).repeat(32)
    a = np.empty((k // 512, 16))
    for p in range(k // 512):
        a[p, :8] = np.random.permutation(np.resize(levels, 8))
        for g in range(8):
            far = levels[np.abs(levels - a[p, g]) >= 10]
            a[p, g + 8] = far[np.random.randint(len(far))]
    return np.exp2(a.ravel()).repeat(32)


def f64(x):
    return np.asarray(x).astype(np.float64)


def striped(idx):
    return np.tile(idx.reshape(-1, 16).T, (8, 1)).astype(np.uint16)


def unstriped(offs):
    return offs[:16].T.reshape(-1).astype(np.int64)


def striped8(idx):
    return np.concatenate([x.reshape(-1, 16).T for x in idx]).astype(np.uint16)


def runs(offs, k):
    lists = np.stack([offs[16 * r : 16 * r + 16].T.reshape(-1) for r in range(8)]).astype(np.int64)
    return lists[np.arange(k) % 512 // 64]


def pack_weight(w):
    k, n = w.shape
    w = f64(np.asarray(w, np.float32).astype(ml_dtypes.bfloat16)).reshape(k // 32, 32, n)
    amax = np.abs(w).max(1)
    byte = np.clip(np.where(amax > 0, np.frexp(amax)[1] - 1 + 127 - 7, 1), 1, 254)
    scaled = (w * np.exp2(127.0 - byte)[:, None, :]).reshape(k, n).astype(np.float32)
    words = np.ascontiguousarray(scaled.reshape(k // 512, 128, 4, n).transpose(0, 1, 3, 2)).astype(ml_dtypes.float8_e4m3fn).view(np.uint8)
    return words, np.ascontiguousarray(byte.astype(np.uint8).reshape(k // 512, 16, n))


def unpack_weight(words, scales):
    g, p, n, _ = words.shape
    vals = np.ascontiguousarray(words).view(ml_dtypes.float8_e4m3fn).astype(np.float64) * np.repeat(np.exp2(scales.astype(np.float64) - 127.0), 8, axis=1)[..., None]
    return vals.transpose(0, 1, 3, 2).reshape(g * 512, n)


def sigmoid(v):
    return 1.0 / (1.0 + np.exp(-np.maximum(v, -700.0)))


K, T, S, H, G, W = 512, 1024, 256, 512, 2048, 128


def setup_inputs():
    n = np.random.standard_normal
    s = mx_kscale(K)[:, None]
    packed_xT = pack_weight(n((K, T)) * s)
    packed_dT = pack_weight(n((K, G)) / s)
    perm = np.random.permutation(S)
    perm2 = np.random.permutation(S)
    return {
        "x_words": packed_xT[0],
        "x_scales": packed_xT[1],
        "w1": (n((K, H)) / np.sqrt(2 * K) / s).astype(np.float32),
        "w2": (n((K, H)) / np.sqrt(2 * K) / s).astype(np.float32),
        "sl": np.random.uniform(1.0, 2.0, (H, 1)).astype(np.float32),
        "th": (0.5 * n((H, 1))).astype(np.float32),
        "gs": (np.random.uniform(0.5, 1.5, (K, 1)) * s).astype(np.float32),
        "d_words": packed_dT[0],
        "d_scales": packed_dT[1],
        "offs": striped(np.random.permutation(T)[:S]),
        "two": striped(np.random.permutation(T)[:S]),
        "n1": striped(np.random.permutation(S)),
        "n2": striped(np.random.permutation(S)),
        "n3": striped(np.random.permutation(S)),
        "k1": striped8(np.random.randint(0, G, (8, H))),
        "k2": striped8(np.random.randint(0, G, (8, H))),
        "hz": striped8(np.random.randint(0, T, (8, S))),
        "n4": striped(perm[:W]),
        "n5": striped(perm[W:]),
        "n6": striped(perm2[:W]),
        "n7": striped(perm2[W:]),
        "n8": striped(np.random.permutation(S)),
    }


def reference(x_words, x_scales, w1, w2, sl, th, gs, d_words, d_scales, offs, two, n1, n2, n3, k1, k2, hz, n4, n5, n6, n7, n8):
    d_k1 = unpack_weight(d_words, d_scales)[np.arange(K)[:, None], runs(k1, K)]
    xq = unpack_weight(x_words, x_scales)[:, unstriped(offs)]
    x_two = unpack_weight(x_words, x_scales)[:, unstriped(two)]
    y = mxq(f64(w1), 0, "e4m3").T @ xq + mxq(f64(w2), 0, "e4m3").T @ x_two
    ds2 = np.zeros((H, S))
    ds2[:, unstriped(n2)] = y
    ds = np.zeros((H, S))
    ds[:, unstriped(n1)] = y
    sg = sigmoid(f64(sl) * (ds[:, unstriped(n3)] - f64(th)))
    z = f64(gs) * (ds2 * sg)
    d_k2 = unpack_weight(d_words, d_scales)[np.arange(K)[:, None], runs(k2, K)]
    x_hz = unpack_weight(x_words, x_scales)[np.arange(K)[:, None], runs(hz, K)]
    h2 = 0.0625 * ((d_k1.T @ mxq(z, 0, "e4m3") + d_k2.T @ x_hz))
    pa = h2[:, unstriped(n4)]
    pb = h2[:, unstriped(n5)]
    rb = np.minimum(pa, pb)
    ra = pa - pb
    ua = np.zeros((H, S))
    ua[:, unstriped(n6)] = ra
    ub = ua.copy()
    ub[:, unstriped(n7)] = rb
    return np.maximum(ub, ub[:, unstriped(n8)])

@@ -1,0 +1,277 @@
+from contextlib import ExitStack
+
+import concourse.mybir as mybir
+
+F32 = mybir.dt.float32
+BF16 = mybir.dt.bfloat16
+I32 = mybir.dt.int32
+U32 = mybir.dt.uint32
+U16 = mybir.dt.uint16
+U8 = mybir.dt.uint8
+FP8X4 = mybir.dt.float8_e4m3fn_x4
+ALU = mybir.AluOpType
+ACT = mybir.ActivationFunctionType
+
+P = 128
+T, S, H, G, W = 1024, 256, 512, 2048, 128
+HALF = 64
+WIDE = 512
+UB = 288
+FLOPS = 4 * 2 * 512 * 512 * 256
+
+
+def tile_picked_dttzmhesntwcpgf_none_p_kernel(
+    tc, x_words, x_scales, w1, w2, sl, th, gs, d_words, d_scales,
+    offs, two, n1, n2, n3, k1, k2, hz, n4, n5, n6, n7, n8, out,
+):
+    nc = tc.nc
+    with ExitStack() as ctx:
+        held = ctx.enter_context(tc.tile_pool(name="held", bufs=1))
+        reused = ctx.enter_context(tc.tile_pool(name="reused", bufs=1))
+        psum = ctx.enter_context(tc.psum_pool(name="psum", bufs=1))
+
+        def sb(name, shape, dtype):
+            return held.tile(shape, dtype, name=name, align_bytes=64)
+
+        def over_words(name, shape, dtype, offset):
+            return reused.tile(shape, dtype, name=name, align_bytes=64, offset=offset)
+
+        def load_list(name, src):
+            t = sb(name, list(src.shape), U16)
+            nc.sync.dma_start(t[:], src)
+            return t
+
+        def load_words(t, src, queue):
+            queue.dma_start(t[:].bitcast(I32), src[0].rearrange("p n t -> p (n t)").bitcast(I32))
+            return t
+
+        def load_scale_row(t, src, r, at, queue):
+            queue.dma_start(t[at:P:32, :].bitcast(I32), src[0].bitcast(I32)[r:16:4, :])
+
+        def load_w_half(name, w, h, queue):
+            t = sb(name, [P, 4, 256], F32)
+            queue.dma_start(t[:], w.rearrange("(p j) c -> p j c", j=4)[:, :, 256 * h : 256 * (h + 1)])
+            return t
+
+        def gather(dst, window, lst):
+            nc.vector.tensor_copy(dst, window[:].indirect(lst))
+
+        def mm(acc, lhs, rhs, start, stop):
+            nc.tensor.matmul_mx(acc, lhsT=lhs[0].bitcast(FP8X4), lhsT_scale=lhs[1], rhs=rhs[0].bitcast(FP8X4), rhs_scale=rhs[1], start=start, stop=stop)
+
+        def quantize(name, src, n):
+            codes = sb(name + "_c", [P, n], U32)
+            plane = sb(name + "_s", [P, n], U8)
+            nc.vector.quantize_mx(codes[:].bitcast(FP8X4), plane[:], src)
+            return codes, plane
+
+        xs = sb("xs", [P, T], U8)
+        nc.gpsimd.memset(xs[:].bitcast(I32), 0)
+        l_offs = load_list("l_offs", offs)
+        l_two = load_list("l_two", two)
+        for r in range(4):
+            load_scale_row(xs, x_scales, r, r, nc.scalar if r < 2 else nc.sync)
+        xw = load_words(sb("xw", [P, T], U32), x_words, nc.sync)
+        raw = {}
+        raw[0, 0] = load_w_half("w1h0", w1, 0, nc.sync)
+        raw[1, 0] = load_w_half("w2h0", w2, 0, nc.sync)
+        xq_c = sb("xq_c", [P, 2 * S], U32)
+        xq_s = sb("xq_s", [P, 2 * S], U8)
+        for a, lst in enumerate((l_offs, l_two)):
+            gather(xq_s[:, a * S : (a + 1) * S], xs, lst[:])
+        for a, lst in enumerate((l_offs, l_two)):
+            gather(xq_c[:, a * S : (a + 1) * S], xw, lst[:])
+        xq = [(xq_c[:, a * S : (a + 1) * S], xq_s[:, a * S : (a + 1) * S]) for a in range(2)]
+        l_n1 = load_list("l_n1", n1)
+        raw[0, 1] = load_w_half("w1h1", w1, 1, nc.sync)
+        raw[1, 1] = load_w_half("w2h1", w2, 1, nc.sync)
+        l_n2 = load_list("l_n2", n2)
+        sl_t = sb("sl_t", [P, 2], F32)
+        th_t = sb("th_t", [P, 2], F32)
+        sl_e = sb("sl_e", [P, 2], F32)
+        th_e = sb("th_e", [P, 2], F32)
+        gs_t = sb("gs_t", [P, 4], F32)
+        with nc.allow_non_contiguous_dma(reason="one value a row"):
+            for dst, src in ((sl_e, sl), (th_e, th)):
+                for r in range(2):
+                    nc.gpsimd.dma_start(dst[HALF * r : HALF * (r + 1), :], src.rearrange("(h m r) o -> r m (h o)", h=2, r=4)[r])
+        l_n3 = load_list("l_n3", n3)
+        for dst, src in ((sl_t, sl), (th_t, th)):
+            nc.sync.dma_start(dst[:], src.rearrange("(p t) o -> p (t o)", t=4)[:, 2:4])
+        for r in (2, 3):
+            load_scale_row(xs, x_scales, r, r + 16, nc.sync)
+        l_hz = load_list("l_hz", hz)
+        dsc = sb("dsc", [P, G], U8)
+        nc.vector.memset(dsc[:].bitcast(I32), 0)
+        for r in range(4):
+            load_scale_row(dsc, d_scales, r, r + 16 * (r // 2), nc.sync)
+        l_k1 = load_list("l_k1", k1)
+        l_k2 = load_list("l_k2", k2)
+        nc.sync.dma_start(gs_t[:], gs.rearrange("(p t) o -> p (t o)", t=4))
+        dw = load_words(over_words("dw", [P, G], U32, 0), d_words, nc.sync)
+
+        ds = [sb("ds%d" % t, [P, WIDE], F32) for t in range(2)] * 2
+        ds2 = [sb("ds2_%d" % t, [P, WIDE], F32) for t in range(4)]
+        ub = [sb("ub%d" % t, [P, UB], F32) for t in range(4)]
+        for t in range(2):
+            nc.vector.memset(ds[t][:, S:], 0.0)
+        for t in range(4):
+            nc.vector.memset(ub[t][:], 0.0)
+
+        l_n4 = load_list("l_n4", n4)
+        l_n5 = load_list("l_n5", n5)
+        l_n6 = load_list("l_n6", n6)
+        l_n7 = load_list("l_n7", n7)
+        l_n8 = load_list("l_n8", n8)
+
+        def w_view(a, h, r0):
+            return raw[a, h][:].rearrange("p j (m r) -> p m r j", r=4)[:, :, r0 : r0 + 2, :]
+
+        ys = []
+
+        def first_product(t, wq):
+            acc = psum.tile([P, S], F32, name="yacc%d" % t, tag="bank%d" % t)
+            for a in range(2):
+                mm(acc[:], wq[a], xq[a], a == 0, a == 1)
+            y = sb("y%d" % t, [P, S], F32)
+            nc.vector.tensor_copy(y[:], acc[:])
+            ys.append(y)
+
+        for h in range(2):
+            wq = []
+            for a in range(2):
+                st = sb("st_e%d%d" % (a, h), [P, 512], BF16)
+                view = st[:].rearrange("p (r m j) -> p m r j", r=2, j=4)
+                if h == 0 and a == 0:
+                    nc.scalar.copy(view, w_view(a, h, 0))
+                elif h == 0:
+                    nc.scalar.copy(view[:, :, 0, :], w_view(a, h, 0)[:, :, 0, :])
+                    nc.vector.tensor_copy(view[:, :, 1, :], w_view(a, h, 0)[:, :, 1, :])
+                else:
+                    nc.vector.tensor_copy(view, w_view(a, h, 0))
+                c, s = quantize("wq_e%d%d" % (a, h), st[:], P)
+                wq.append((c[:], s[:]))
+            first_product(h, wq)
+        late = []
+        for a in range(2):
+            st = sb("st_l%d" % a, [P, 1024], BF16)
+            for h in range(2):
+                nc.vector.tensor_copy(st[:].rearrange("p (r h m j) -> p h m r j", r=2, h=2, j=4)[:, h], w_view(a, h, 2))
+            late.append(quantize("wq_l%d" % a, st[:], 2 * P))
+        for r in range(2):
+            first_product(2 + r, [(c[:, P * r : P * (r + 1)], s[:, P * r : P * (r + 1)]) for c, s in late])
+
+        nb_e = sb("nb_e", [P, 2], F32)
+        nb_t = sb("nb_t", [P, 2], F32)
+        for bias, slope, thr in ((nb_e, sl_e, th_e), (nb_t, sl_t, th_t)):
+            for t in range(2):
+                nc.gpsimd.tensor_scalar(bias[:, t : t + 1], thr[:, t : t + 1], slope[:, t : t + 1], -1.0, ALU.mult, ALU.mult)
+
+        dq_c = sb("dq_c", [P, 2 * H], U32)
+        hz_c = sb("hz_c", [P, S], U32)
+        picked = over_words("picked", [P, 2 * H + S], U8, 4 * G)
+        planes = sb("planes", [P, 2 * H + S], U8)
+        gather(picked[:, 0:H], dsc, l_k1[:])
+        gather(picked[:, H : 2 * H], dsc, l_k2[:])
+        gather(picked[:, 2 * H :], xs, l_hz[:])
+        nc.vector.tensor_copy(planes[:].bitcast(I32), picked[:].bitcast(I32))
+        for r in (2, 3):
+            nc.sync.dma_start(planes[r:P:32, :].bitcast(I32), picked[r + 16 : P : 32, :].bitcast(I32))
+        gather(dq_c[:, 0:H], dw, l_k1[:])
+        gather(dq_c[:, H : 2 * H], dw, l_k2[:])
+        gather(hz_c[:], xw, l_hz[:])
+
+        zb = [over_words("zb%d" % c, [P, W, 4], BF16, 4 * G - 1536 + 1024 * c) for c in range(2)]
+        sg = [sb("sg%d" % t, [P, S], F32) for t in range(3)] + [over_words("sg3", [P, S], F32, 2560)]
+        u = [over_words("u%d" % t, [P, S], F32, 2048 + 1024 * t) for t in range(2)]
+        away = over_words("away", [P, S], F32, 4096)
+        lo, hi = slice(0, HALF), slice(HALF, P)
+
+        def scatter(window, lst, src):
+            nc.scalar.activation(window[:].indirect(lst), src, ACT.Copy)
+
+        def fetch(dst, window, lst):
+            nc.scalar.activation(dst, window[:].indirect(lst), ACT.Copy)
+
+        def gate(t, c0, n, slope, bias):
+            nc.scalar.activation(sg[t][:, c0 : c0 + n], ds[t][:].indirect(l_n3[:, c0 // 16 : (c0 + n) // 16]), ACT.Sigmoid, scale=slope, bias=bias)
+
+        for t in range(2):
+            scatter(ds[t], l_n1[:], ys[t][:])
+            scatter(ds2[t], l_n2[:], ys[t][:])
+            gate(t, 0, S, sl_e[:, t : t + 1], nb_e[:, t : t + 1])
+            stay, go = (lo, hi) if t == 0 else (hi, lo)
+            nc.vector.tensor_tensor(away[go, :], ds2[t][go, 0:S], sg[t][go, :], ALU.mult)
+            nc.sync.dma_start(u[1 - t][stay, :], away[go, :])
+            nc.vector.tensor_tensor(u[t][stay, :], ds2[t][stay, 0:S], sg[t][stay, :], ALU.mult)
+        for t in range(2):
+            for c in range(2):
+                nc.vector.tensor_scalar(zb[c][:, :, t], u[t][:, W * c : W * (c + 1)], gs_t[:, t : t + 1], None, ALU.mult)
+
+        def z_in_place(t, c):
+            cols = slice(W * c, W * (c + 1))
+            nc.vector.scalar_tensor_tensor(zb[c][:, :, t], ds2[t][:, cols], gs_t[:, t : t + 1], sg[t][:, cols], ALU.mult, ALU.mult)
+
+        scatter(ds[2], l_n1[:], ys[2][:])
+        scatter(ds2[2], l_n2[:], ys[2][:])
+        gate(2, 0, S, sl_t[:, 0:1], nb_t[:, 0:1])
+        for c in range(2):
+            z_in_place(2, c)
+        scatter(ds[3], l_n1[:], ys[3][:])
+        scatter(ds2[3], l_n2[:], ys[3][:])
+
+        def coded(a, i):
+            cols = slice(a * H + P * i, a * H + P * (i + 1))
+            return dq_c[:, cols], planes[:, cols]
+
+        def hashed(c):
+            return hz_c[:, W * c : W * (c + 1)], planes[:, 2 * H + W * c : 2 * H + W * (c + 1)]
+
+        hacc = [[psum.tile([P, W], F32, name="hacc%d%d" % (i, c), tag="bank%d" % (4 * c + i)) for c in range(2)] for i in range(4)]
+        h2 = [sb("h2_%d" % i, [P, S], F32) for i in range(4)]
+        for i in range(4):
+            for c in range(2):
+                mm(hacc[i][c][:], coded(1, i), hashed(c), True, False)
+        zq = []
+        for c in range(2):
+            gate(3, W * c, W, sl_t[:, 1:2], nb_t[:, 1:2])
+            z_in_place(3, c)
+            codes, plane = quantize("zq%d" % c, zb[c][:].rearrange("p c t -> p (c t)"), W)
+            zq.append((codes[:], plane[:]))
+        for i in range(4):
+            for c in range(2):
+                mm(hacc[i][c][:], coded(0, i), zq[c], False, True)
+        for i in range(4):
+            nc.vector.tensor_scalar(h2[i][:, 0:W], hacc[i][0][:], 0.0625, None, ALU.mult)
+            if i == 0:
+                nc.scalar.activation(h2[i][:, W:S], hacc[i][1][:], ACT.Copy, scale=0.0625)
+            else:
+                nc.vector.tensor_scalar(h2[i][:, W:S], hacc[i][1][:], 0.0625, None, ALU.mult)
+
+        pab = [sb("pab%d" % i, [P, 2, W], F32) for i in range(4)]
+        rab = [sb("rab%d" % i, [P, 2, W], F32) for i in range(4)]
+        far = [sb("far%d" % i, [P, S], F32) for i in range(4)]
+        res = [sb("res%d" % i, [P, S], F32) for i in range(4)]
+
+        def pair_up(i):
+            fetch(pab[i][:, 0, :], h2[i], l_n4[:])
+            fetch(pab[i][:, 1, :], h2[i], l_n5[:])
+            nc.vector.tensor_tensor(rab[i][:, 0, :], pab[i][:, 0, :], pab[i][:, 1, :], ALU.subtract)
+            nc.vector.tensor_tensor(rab[i][:, 1, :], pab[i][:, 0, :], pab[i][:, 1, :], ALU.min)
+
+        def finish(i, c0, n):
+            cols = slice(c0, c0 + n)
+            fetch(far[i][:, cols], ub[i], l_n8[:, c0 // 16 : (c0 + n) // 16])
+            nc.vector.tensor_tensor(res[i][:, cols], ub[i][:, cols], far[i][:, cols], ALU.max)
+            nc.sync.dma_start(out[P * i : P * (i + 1), cols], res[i][:, cols])
+
+        pair_up(0)
+        for i in range(4):
+            if i + 1 < 4:
+                pair_up(i + 1)
+            scatter(ub[i], l_n6[:], rab[i][:, 0, :])
+            if i > 0:
+                finish(i - 1, 0, S)
+            scatter(ub[i], l_n7[:], rab[i][:, 1, :])
+        finish(3, 0, 192)
+        finish(3, 192, 64)

@@ -75,6 +75,9 @@ def tile_picked_dttzmhesntwcpgf_none_p_kernel(
         raw = {}
         raw[0, 0] = load_w_half("w1h0", w1, 0, nc.sync)
         raw[1, 0] = load_w_half("w2h0", w2, 0, nc.sync)
+        warm = sb("warm", [P, 2], F32)
+        nc.gpsimd.memset(warm[:, 0:1], 0.0)
+        nc.scalar.activation(warm[:, 1:2], warm[:, 0:1], ACT.Sigmoid)
         xq_c = sb("xq_c", [P, 2 * S], U32)
         xq_s = sb("xq_s", [P, 2 * S], U8)
         for a, lst in enumerate((l_offs, l_two)):

@@ -69,9 +69,9 @@ def tile_picked_dttzmhesntwcpgf_none_p_kernel(
         nc.gpsimd.memset(xs[:].bitcast(I32), 0)
         l_offs = load_list("l_offs", offs)
         l_two = load_list("l_two", two)
+        xw = load_words(sb("xw", [P, T], U32), x_words, nc.sync)
         for r in range(4):
             load_scale_row(xs, x_scales, r, r, nc.scalar if r < 2 else nc.sync)
-        xw = load_words(sb("xw", [P, T], U32), x_words, nc.sync)
         raw = {}
         raw[0, 0] = load_w_half("w1h0", w1, 0, nc.sync)
         raw[1, 0] = load_w_half("w2h0", w2, 0, nc.sync)
@@ -81,14 +81,14 @@ def tile_picked_dttzmhesntwcpgf_none_p_kernel(
         xq_c = sb("xq_c", [P, 2 * S], U32)
         xq_s = sb("xq_s", [P, 2 * S], U8)
         for a, lst in enumerate((l_offs, l_two)):
-            gather(xq_s[:, a * S : (a + 1) * S], xs, lst[:])
-        for a, lst in enumerate((l_offs, l_two)):
             gather(xq_c[:, a * S : (a + 1) * S], xw, lst[:])
-        xq = [(xq_c[:, a * S : (a + 1) * S], xq_s[:, a * S : (a + 1) * S]) for a in range(2)]
+        for a, lst in enumerate((l_offs, l_two)):
+            gather(xq_s[:, a * S : (a + 1) * S], xs, lst[:])
         l_n1 = load_list("l_n1", n1)
+        l_n2 = load_list("l_n2", n2)
+        l_n3 = load_list("l_n3", n3)
         raw[0, 1] = load_w_half("w1h1", w1, 1, nc.sync)
         raw[1, 1] = load_w_half("w2h1", w2, 1, nc.sync)
-        l_n2 = load_list("l_n2", n2)
         sl_t = sb("sl_t", [P, 2], F32)
         th_t = sb("th_t", [P, 2], F32)
         sl_e = sb("sl_e", [P, 2], F32)
@@ -98,7 +98,6 @@ def tile_picked_dttzmhesntwcpgf_none_p_kernel(
             for dst, src in ((sl_e, sl), (th_e, th)):
                 for r in range(2):
                     nc.gpsimd.dma_start(dst[HALF * r : HALF * (r + 1), :], src.rearrange("(h m r) o -> r m (h o)", h=2, r=4)[r])
-        l_n3 = load_list("l_n3", n3)
         for dst, src in ((sl_t, sl), (th_t, th)):
             nc.sync.dma_start(dst[:], src.rearrange("(p t) o -> p (t o)", t=4)[:, 2:4])
         for r in (2, 3):
@@ -132,12 +131,16 @@ def tile_picked_dttzmhesntwcpgf_none_p_kernel(
 
         ys = []
 
-        def first_product(t, wq):
-            acc = psum.tile([P, S], F32, name="yacc%d" % t, tag="bank%d" % t)
+        def first_product(t, wq, pieces):
+            n = S // pieces
+            accs = [psum.tile([P, n], F32, name="yacc%d%d" % (t, c), tag="bank%d" % (t + 4 * c)) for c in range(pieces)]
             for a in range(2):
-                mm(acc[:], wq[a], xq[a], a == 0, a == 1)
+                for c in range(pieces):
+                    cols = slice(a * S + c * n, a * S + (c + 1) * n)
+                    mm(accs[c][:], wq[a], (xq_c[:, cols], xq_s[:, cols]), a == 0, a == 1)
             y = sb("y%d" % t, [P, S], F32)
-            nc.vector.tensor_copy(y[:], acc[:])
+            for c in range(pieces):
+                nc.vector.tensor_copy(y[:, c * n : (c + 1) * n], accs[c][:])
             ys.append(y)
 
         for h in range(2):
@@ -154,7 +157,7 @@ def tile_picked_dttzmhesntwcpgf_none_p_kernel(
                     nc.vector.tensor_copy(view, w_view(a, h, 0))
                 c, s = quantize("wq_e%d%d" % (a, h), st[:], P)
                 wq.append((c[:], s[:]))
-            first_product(h, wq)
+            first_product(h, wq, 2 - h)
         late = []
         for a in range(2):
             st = sb("st_l%d" % a, [P, 1024], BF16)
@@ -162,7 +165,7 @@ def tile_picked_dttzmhesntwcpgf_none_p_kernel(
                 nc.vector.tensor_copy(st[:].rearrange("p (r h m j) -> p h m r j", r=2, h=2, j=4)[:, h], w_view(a, h, 2))
             late.append(quantize("wq_l%d" % a, st[:], 2 * P))
         for r in range(2):
-            first_product(2 + r, [(c[:, P * r : P * (r + 1)], s[:, P * r : P * (r + 1)]) for c, s in late])
+            first_product(2 + r, [(c[:, P * r : P * (r + 1)], s[:, P * r : P * (r + 1)]) for c, s in late], 1)
 
         nb_e = sb("nb_e", [P, 2], F32)
         nb_t = sb("nb_t", [P, 2], F32)
@@ -200,7 +203,11 @@ def tile_picked_dttzmhesntwcpgf_none_p_kernel(
             nc.scalar.activation(sg[t][:, c0 : c0 + n], ds[t][:].indirect(l_n3[:, c0 // 16 : (c0 + n) // 16]), ACT.Sigmoid, scale=slope, bias=bias)
 
         for t in range(2):
-            scatter(ds[t], l_n1[:], ys[t][:])
+            if t == 0:
+                for c in range(2):
+                    scatter(ds[t], l_n1[:, 8 * c : 8 * (c + 1)], ys[t][:, W * c : W * (c + 1)])
+            else:
+                scatter(ds[t], l_n1[:], ys[t][:])
             scatter(ds2[t], l_n2[:], ys[t][:])
             gate(t, 0, S, sl_e[:, t : t + 1], nb_e[:, t : t + 1])
             stay, go = (lo, hi) if t == 0 else (hi, lo)
@@ -239,6 +246,7 @@ def tile_picked_dttzmhesntwcpgf_none_p_kernel(
         for c in range(2):
             gate(3, W * c, W, sl_t[:, 1:2], nb_t[:, 1:2])
             z_in_place(3, c)
+        for c in range(2):
             codes, plane = quantize("zq%d" % c, zb[c][:].rearrange("p c t -> p (c t)"), W)
             zq.append((codes[:], plane[:]))
         for i in range(4):
@@ -268,13 +276,15 @@ def tile_picked_dttzmhesntwcpgf_none_p_kernel(
             nc.vector.tensor_tensor(res[i][:, cols], ub[i][:, cols], far[i][:, cols], ALU.max)
             nc.sync.dma_start(out[P * i : P * (i + 1), cols], res[i][:, cols])
 
-        pair_up(0)
-        for i in range(4):
-            if i + 1 < 4:
-                pair_up(i + 1)
-            scatter(ub[i], l_n6[:], rab[i][:, 0, :])
-            if i > 0:
-                finish(i - 1, 0, S)
-            scatter(ub[i], l_n7[:], rab[i][:, 1, :])
+        for i0 in (0, 2):
+            pair_up(i0)
+            pair_up(i0 + 1)
+            if i0 > 0:
+                finish(0, 0, S)
+                finish(1, 0, S)
+            for lst, a in ((l_n6, 0), (l_n7, 1)):
+                for i in (i0, i0 + 1):
+                    scatter(ub[i], lst[:], rab[i][:, a, :])
+        finish(2, 0, S)
         finish(3, 0, 192)
         finish(3, 192, 64)

@@ -103,7 +103,7 @@ def tile_picked_dttzmhesntwcpgf_none_p_kernel(
         for r in (2, 3):
             load_scale_row(xs, x_scales, r, r + 16, nc.sync)
         l_hz = load_list("l_hz", hz)
-        dsc = sb("dsc", [P, G], U8)
+        dsc = over_words("dsc", [P, G], U8, 9472)
         nc.vector.memset(dsc[:].bitcast(I32), 0)
         for r in range(4):
             load_scale_row(dsc, d_scales, r, r + 16 * (r // 2), nc.sync)
@@ -188,9 +188,9 @@ def tile_picked_dttzmhesntwcpgf_none_p_kernel(
         gather(hz_c[:], xw, l_hz[:])
 
         zb = [over_words("zb%d" % c, [P, W, 4], BF16, 4 * G - 1536 + 1024 * c) for c in range(2)]
-        sg = [sb("sg%d" % t, [P, S], F32) for t in range(3)] + [over_words("sg3", [P, S], F32, 2560)]
-        u = [over_words("u%d" % t, [P, S], F32, 2048 + 1024 * t) for t in range(2)]
-        away = over_words("away", [P, S], F32, 4096)
+        sg = [sb("sg%d" % t, [P, S], F32) for t in range(3)] + [over_words("sg3", [P, S], F32, 9984)]
+        u = [over_words("u%d" % t, [P, S], F32, 9472 + 1024 * t) for t in range(2)]
+        away = sb("away", [P, S], F32)
         lo, hi = slice(0, HALF), slice(HALF, P)
 
         def scatter(window, lst, src):
@@ -211,9 +211,9 @@ def tile_picked_dttzmhesntwcpgf_none_p_kernel(
             scatter(ds2[t], l_n2[:], ys[t][:])
             gate(t, 0, S, sl_e[:, t : t + 1], nb_e[:, t : t + 1])
             stay, go = (lo, hi) if t == 0 else (hi, lo)
-            nc.vector.tensor_tensor(away[go, :], ds2[t][go, 0:S], sg[t][go, :], ALU.mult)
+            nc.gpsimd.tensor_tensor(away[go, :], ds2[t][go, 0:S], sg[t][go, :], ALU.mult)
             nc.sync.dma_start(u[1 - t][stay, :], away[go, :])
-            nc.vector.tensor_tensor(u[t][stay, :], ds2[t][stay, 0:S], sg[t][stay, :], ALU.mult)
+            nc.gpsimd.tensor_tensor(u[t][stay, :], ds2[t][stay, 0:S], sg[t][stay, :], ALU.mult)
         for t in range(2):
             for c in range(2):
                 nc.vector.tensor_scalar(zb[c][:, :, t], u[t][:, W * c : W * (c + 1)], gs_t[:, t : t + 1], None, ALU.mult)

from contextlib import ExitStack

import concourse.mybir as mybir

F32 = mybir.dt.float32
BF16 = mybir.dt.bfloat16
I32 = mybir.dt.int32
U32 = mybir.dt.uint32
U16 = mybir.dt.uint16
U8 = mybir.dt.uint8
FP8X4 = mybir.dt.float8_e4m3fn_x4
ALU = mybir.AluOpType
ACT = mybir.ActivationFunctionType

P = 128
T, S, H, G, W = 1024, 256, 512, 2048, 128
HALF = 64
WIDE = 512
UB = 288
FLOPS = 4 * 2 * 512 * 512 * 256


def tile_picked_dttzmhesntwcpgf_none_p_kernel(
    tc, x_words, x_scales, w1, w2, sl, th, gs, d_words, d_scales,
    offs, two, n1, n2, n3, k1, k2, hz, n4, n5, n6, n7, n8, out,
):
    nc = tc.nc
    with ExitStack() as ctx:
        held = ctx.enter_context(tc.tile_pool(name="held", bufs=1))
        reused = ctx.enter_context(tc.tile_pool(name="reused", bufs=1))
        psum = ctx.enter_context(tc.psum_pool(name="psum", bufs=1))

        def sb(name, shape, dtype):
            return held.tile(shape, dtype, name=name, align_bytes=64)

        def over_words(name, shape, dtype, offset):
            return reused.tile(shape, dtype, name=name, align_bytes=64, offset=offset)

        def load_list(name, src):
            t = sb(name, list(src.shape), U16)
            nc.sync.dma_start(t[:], src)
            return t

        def load_words(t, src, queue):
            queue.dma_start(t[:].bitcast(I32), src[0].rearrange("p n t -> p (n t)").bitcast(I32))
            return t

        def load_scale_row(t, src, r, at, queue):
            queue.dma_start(t[at:P:32, :].bitcast(I32), src[0].bitcast(I32)[r:16:4, :])

        def load_w_half(name, w, h, queue):
            t = sb(name, [P, 4, 256], F32)
            queue.dma_start(t[:], w.rearrange("(p j) c -> p j c", j=4)[:, :, 256 * h : 256 * (h + 1)])
            return t

        def gather(dst, window, lst):
            nc.vector.tensor_copy(dst, window[:].indirect(lst))

        def mm(acc, lhs, rhs, start, stop):
            nc.tensor.matmul_mx(acc, lhsT=lhs[0].bitcast(FP8X4), lhsT_scale=lhs[1], rhs=rhs[0].bitcast(FP8X4), rhs_scale=rhs[1], start=start, stop=stop)

        def quantize(name, src, n):
            codes = sb(name + "_c", [P, n], U32)
            plane = sb(name + "_s", [P, n], U8)
            nc.vector.quantize_mx(codes[:].bitcast(FP8X4), plane[:], src)
            return codes, plane

        xs = sb("xs", [P, T], U8)
        nc.gpsimd.memset(xs[:].bitcast(I32), 0)
        l_offs = load_list("l_offs", offs)
        l_two = load_list("l_two", two)
        xw = load_words(sb("xw", [P, T], U32), x_words, nc.sync)
        for r in range(4):
            load_scale_row(xs, x_scales, r, r, nc.scalar if r < 2 else nc.sync)
        raw = {}
        raw[0, 0] = load_w_half("w1h0", w1, 0, nc.sync)
        raw[1, 0] = load_w_half("w2h0", w2, 0, nc.sync)
        warm = sb("warm", [P, 2], F32)
        nc.gpsimd.memset(warm[:, 0:1], 0.0)
        nc.scalar.activation(warm[:, 1:2], warm[:, 0:1], ACT.Sigmoid)
        xq_c = sb("xq_c", [P, 2 * S], U32)
        xq_s = sb("xq_s", [P, 2 * S], U8)
        for a, lst in enumerate((l_offs, l_two)):
            gather(xq_c[:, a * S : (a + 1) * S], xw, lst[:])
        for a, lst in enumerate((l_offs, l_two)):
            gather(xq_s[:, a * S : (a + 1) * S], xs, lst[:])
        l_n1 = load_list("l_n1", n1)
        l_n2 = load_list("l_n2", n2)
        l_n3 = load_list("l_n3", n3)
        raw[0, 1] = load_w_half("w1h1", w1, 1, nc.sync)
        raw[1, 1] = load_w_half("w2h1", w2, 1, nc.sync)
        sl_t = sb("sl_t", [P, 2], F32)
        th_t = sb("th_t", [P, 2], F32)
        sl_e = sb("sl_e", [P, 2], F32)
        th_e = sb("th_e", [P, 2], F32)
        gs_t = sb("gs_t", [P, 4], F32)
        with nc.allow_non_contiguous_dma(reason="one value a row"):
            for dst, src in ((sl_e, sl), (th_e, th)):
                for r in range(2):
                    nc.gpsimd.dma_start(dst[HALF * r : HALF * (r + 1), :], src.rearrange("(h m r) o -> r m (h o)", h=2, r=4)[r])
        for dst, src in ((sl_t, sl), (th_t, th)):
            nc.sync.dma_start(dst[:], src.rearrange("(p t) o -> p (t o)", t=4)[:, 2:4])
        for r in (2, 3):
            load_scale_row(xs, x_scales, r, r + 16, nc.sync)
        l_hz = load_list("l_hz", hz)
        dsc = over_words("dsc", [P, G], U8, 9472)
        nc.vector.memset(dsc[:].bitcast(I32), 0)
        for r in range(4):
            load_scale_row(dsc, d_scales, r, r + 16 * (r // 2), nc.sync)
        l_k1 = load_list("l_k1", k1)
        l_k2 = load_list("l_k2", k2)
        nc.sync.dma_start(gs_t[:], gs.rearrange("(p t) o -> p (t o)", t=4))
        dw = load_words(over_words("dw", [P, G], U32, 0), d_words, nc.sync)

        ds = [sb("ds%d" % t, [P, WIDE], F32) for t in range(2)] * 2
        ds2 = [sb("ds2_%d" % t, [P, WIDE], F32) for t in range(4)]
        ub = [sb("ub%d" % t, [P, UB], F32) for t in range(4)]
        for t in range(2):
            nc.vector.memset(ds[t][:, S:], 0.0)
        for t in range(4):
            nc.vector.memset(ub[t][:], 0.0)

        l_n4 = load_list("l_n4", n4)
        l_n5 = load_list("l_n5", n5)
        l_n6 = load_list("l_n6", n6)
        l_n7 = load_list("l_n7", n7)
        l_n8 = load_list("l_n8", n8)

        def w_view(a, h, r0):
            return raw[a, h][:].rearrange("p j (m r) -> p m r j", r=4)[:, :, r0 : r0 + 2, :]

        ys = []

        def first_product(t, wq, pieces):
            n = S // pieces
            accs = [psum.tile([P, n], F32, name="yacc%d%d" % (t, c), tag="bank%d" % (t + 4 * c)) for c in range(pieces)]
            for a in range(2):
                for c in range(pieces):
                    cols = slice(a * S + c * n, a * S + (c + 1) * n)
                    mm(accs[c][:], wq[a], (xq_c[:, cols], xq_s[:, cols]), a == 0, a == 1)
            y = sb("y%d" % t, [P, S], F32)
            for c in range(pieces):
                nc.vector.tensor_copy(y[:, c * n : (c + 1) * n], accs[c][:])
            ys.append(y)

        for h in range(2):
            wq = []
            for a in range(2):
                st = sb("st_e%d%d" % (a, h), [P, 512], BF16)
                view = st[:].rearrange("p (r m j) -> p m r j", r=2, j=4)
                if h == 0 and a == 0:
                    nc.scalar.copy(view, w_view(a, h, 0))
                elif h == 0:
                    nc.scalar.copy(view[:, :, 0, :], w_view(a, h, 0)[:, :, 0, :])
                    nc.vector.tensor_copy(view[:, :, 1, :], w_view(a, h, 0)[:, :, 1, :])
                else:
                    nc.vector.tensor_copy(view, w_view(a, h, 0))
                c, s = quantize("wq_e%d%d" % (a, h), st[:], P)
                wq.append((c[:], s[:]))
            first_product(h, wq, 2 - h)
        late = []
        for a in range(2):
            st = sb("st_l%d" % a, [P, 1024], BF16)
            for h in range(2):
                nc.vector.tensor_copy(st[:].rearrange("p (r h m j) -> p h m r j", r=2, h=2, j=4)[:, h], w_view(a, h, 2))
            late.append(quantize("wq_l%d" % a, st[:], 2 * P))
        for r in range(2):
            first_product(2 + r, [(c[:, P * r : P * (r + 1)], s[:, P * r : P * (r + 1)]) for c, s in late], 1)

        nb_e = sb("nb_e", [P, 2], F32)
        nb_t = sb("nb_t", [P, 2], F32)
        for bias, slope, thr in ((nb_e, sl_e, th_e), (nb_t, sl_t, th_t)):
            for t in range(2):
                nc.gpsimd.tensor_scalar(bias[:, t : t + 1], thr[:, t : t + 1], slope[:, t : t + 1], -1.0, ALU.mult, ALU.mult)

        dq_c = sb("dq_c", [P, 2 * H], U32)
        hz_c = sb("hz_c", [P, S], U32)
        picked = over_words("picked", [P, 2 * H + S], U8, 4 * G)
        planes = sb("planes", [P, 2 * H + S], U8)
        gather(picked[:, 0:H], dsc, l_k1[:])
        gather(picked[:, H : 2 * H], dsc, l_k2[:])
        gather(picked[:, 2 * H :], xs, l_hz[:])
        nc.vector.tensor_copy(planes[:].bitcast(I32), picked[:].bitcast(I32))
        for r in (2, 3):
            nc.sync.dma_start(planes[r:P:32, :].bitcast(I32), picked[r + 16 : P : 32, :].bitcast(I32))
        gather(dq_c[:, 0:H], dw, l_k1[:])
        gather(dq_c[:, H : 2 * H], dw, l_k2[:])
        gather(hz_c[:], xw, l_hz[:])

        zb = [over_words("zb%d" % c, [P, W, 4], BF16, 4 * G - 1536 + 1024 * c) for c in range(2)]
        sg = [sb("sg%d" % t, [P, S], F32) for t in range(3)] + [over_words("sg3", [P, S], F32, 9984)]
        u = [over_words("u%d" % t, [P, S], F32, 9472 + 1024 * t) for t in range(2)]
        away = sb("away", [P, S], F32)
        lo, hi = slice(0, HALF), slice(HALF, P)

        def scatter(window, lst, src):
            nc.scalar.activation(window[:].indirect(lst), src, ACT.Copy)

        def fetch(dst, window, lst):
            nc.scalar.activation(dst, window[:].indirect(lst), ACT.Copy)

        def gate(t, c0, n, slope, bias):
            nc.scalar.activation(sg[t][:, c0 : c0 + n], ds[t][:].indirect(l_n3[:, c0 // 16 : (c0 + n) // 16]), ACT.Sigmoid, scale=slope, bias=bias)

        for t in range(2):
            if t == 0:
                for c in range(2):
                    scatter(ds[t], l_n1[:, 8 * c : 8 * (c + 1)], ys[t][:, W * c : W * (c + 1)])
            else:
                scatter(ds[t], l_n1[:], ys[t][:])
            scatter(ds2[t], l_n2[:], ys[t][:])
            gate(t, 0, S, sl_e[:, t : t + 1], nb_e[:, t : t + 1])
            stay, go = (lo, hi) if t == 0 else (hi, lo)
            nc.gpsimd.tensor_tensor(away[go, :], ds2[t][go, 0:S], sg[t][go, :], ALU.mult)
            nc.sync.dma_start(u[1 - t][stay, :], away[go, :])
            nc.gpsimd.tensor_tensor(u[t][stay, :], ds2[t][stay, 0:S], sg[t][stay, :], ALU.mult)
        for t in range(2):
            for c in range(2):
                nc.vector.tensor_scalar(zb[c][:, :, t], u[t][:, W * c : W * (c + 1)], gs_t[:, t : t + 1], None, ALU.mult)

        def z_in_place(t, c):
            cols = slice(W * c, W * (c + 1))
            nc.vector.scalar_tensor_tensor(zb[c][:, :, t], ds2[t][:, cols], gs_t[:, t : t + 1], sg[t][:, cols], ALU.mult, ALU.mult)

        scatter(ds[2], l_n1[:], ys[2][:])
        scatter(ds2[2], l_n2[:], ys[2][:])
        gate(2, 0, S, sl_t[:, 0:1], nb_t[:, 0:1])
        for c in range(2):
            z_in_place(2, c)
        scatter(ds[3], l_n1[:], ys[3][:])
        scatter(ds2[3], l_n2[:], ys[3][:])

        def coded(a, i):
            cols = slice(a * H + P * i, a * H + P * (i + 1))
            return dq_c[:, cols], planes[:, cols]

        def hashed(c):
            return hz_c[:, W * c : W * (c + 1)], planes[:, 2 * H + W * c : 2 * H + W * (c + 1)]

        hacc = [[psum.tile([P, W], F32, name="hacc%d%d" % (i, c), tag="bank%d" % (4 * c + i)) for c in range(2)] for i in range(4)]
        h2 = [sb("h2_%d" % i, [P, S], F32) for i in range(4)]
        for i in range(4):
            for c in range(2):
                mm(hacc[i][c][:], coded(1, i), hashed(c), True, False)
        zq = []
        for c in range(2):
            gate(3, W * c, W, sl_t[:, 1:2], nb_t[:, 1:2])
            z_in_place(3, c)
        for c in range(2):
            codes, plane = quantize("zq%d" % c, zb[c][:].rearrange("p c t -> p (c t)"), W)
            zq.append((codes[:], plane[:]))
        for i in range(4):
            for c in range(2):
                mm(hacc[i][c][:], coded(0, i), zq[c], False, True)
        for i in range(4):
            nc.vector.tensor_scalar(h2[i][:, 0:W], hacc[i][0][:], 0.0625, None, ALU.mult)
            if i == 0:
                nc.scalar.activation(h2[i][:, W:S], hacc[i][1][:], ACT.Copy, scale=0.0625)
            else:
                nc.vector.tensor_scalar(h2[i][:, W:S], hacc[i][1][:], 0.0625, None, ALU.mult)

        pab = [sb("pab%d" % i, [P, 2, W], F32) for i in range(4)]
        rab = [sb("rab%d" % i, [P, 2, W], F32) for i in range(4)]
        far = [sb("far%d" % i, [P, S], F32) for i in range(4)]
        res = [sb("res%d" % i, [P, S], F32) for i in range(4)]

        def pair_up(i):
            fetch(pab[i][:, 0, :], h2[i], l_n4[:])
            fetch(pab[i][:, 1, :], h2[i], l_n5[:])
            nc.vector.tensor_tensor(rab[i][:, 0, :], pab[i][:, 0, :], pab[i][:, 1, :], ALU.subtract)
            nc.vector.tensor_tensor(rab[i][:, 1, :], pab[i][:, 0, :], pab[i][:, 1, :], ALU.min)

        def finish(i, c0, n):
            cols = slice(c0, c0 + n)
            fetch(far[i][:, cols], ub[i], l_n8[:, c0 // 16 : (c0 + n) // 16])
            nc.vector.tensor_tensor(res[i][:, cols], ub[i][:, cols], far[i][:, cols], ALU.max)
            nc.sync.dma_start(out[P * i : P * (i + 1), cols], res[i][:, cols])

        for i0 in (0, 2):
            pair_up(i0)
            pair_up(i0 + 1)
            if i0 > 0:
                finish(0, 0, S)
                finish(1, 0, S)
            for lst, a in ((l_n6, 0), (l_n7, 1)):
                for i in (i0, i0 + 1):
                    scatter(ub[i], lst[:], rab[i][:, a, :])
        finish(2, 0, S)
        finish(3, 0, 192)
        finish(3, 192, 64)
